import numpy as np
import ml_dtypes


def mxq(x, axis, fmt="e4m3"):
    dtype, down = {"e4m3": (ml_dtypes.float8_e4m3fn, 7), "e5m2": (ml_dtypes.float8_e5m2, 14)}[fmt]
    v = np.moveaxis(np.asarray(x, np.float32).astype(ml_dtypes.bfloat16).astype(np.float64), axis, -1)
    blocks = v.reshape(v.shape[:-1] + (-1, 32))
    amax = np.abs(blocks).max(-1, keepdims=True)
    byte = np.maximum(np.where(amax > 0, np.frexp(amax)[1] - 1 + 127, 0) - down, 1)
    scale = np.exp2(byte - 127.0)
    codes = (blocks / scale).astype(np.float32).astype(dtype).astype(np.float64)
    return np.moveaxis((codes * scale).reshape(v.shape), -1, axis)


WIDE = False


def mx_kscale(k, group=512):
    if not WIDE:
        return np.ones(k)
    levels = np.array([10, -10, 5, -5, 0])
    if group != 512:
        return np.exp2(np.random.permutation(np.resize(levels, k // group))).repeat(group)
    if k % 512:
        return np.exp2(np.random.permutation(np.resize(levels, k // 32))).repeat(32)
    a = np.empty((k // 512, 16))
    for p in range(k // 512):
        a[p, :8] = np.random.permutation(np.resize(levels, 8))
        for g in range(8):
            far = levels[np.abs(levels - a[p, g]) >= 10]
            a[p, g + 8] = far[np.random.randint(len(far))]
    return np.exp2(a.ravel()).repeat(32)


def f64(x):
    return np.asarray(x).astype(np.float64)


def bf(x):
    return np.asarray(x, np.float32).astype(ml_dtypes.bfloat16)


def planes(Y):
    r, m = Y.shape
    b = f64(bf(Y)).reshape(r // 32, 32, m)
    amax = np.abs(b).max(1)
    byte = np.clip(np.where(amax > 0, np.frexp(amax)[1] - 1 + 127 - 7, 1), 1, 254)
    codes = (b * np.exp2(127.0 - byte)[:, None, :]).reshape(r, m).astype(np.float32).astype(ml_dtypes.float8_e4m3fn).view(np.uint8)
    words = codes.reshape(r // 512, 128, 4, m).transpose(0, 1, 3, 2)
    return np.ascontiguousarray(words), np.ascontiguousarray(byte.astype(np.uint8).reshape(r // 512, 16, m))


G, D, M, N = 2, 256, 256, 512


def setup_inputs():
    n = np.random.standard_normal
    s_d = mx_kscale(D, 0)
    return {
        "x": (n((G, D, N)) * s_d[:, None]).astype(np.float32),
        "w1": (n((G, D, M)) / np.sqrt(D) / s_d[:, None]).astype(np.float32),
        "w2": (n((G, D, M)) / np.sqrt(D) / s_d[:, None]).astype(np.float32),
        "tp": (np.random.uniform(0.5, 1.2, (G, M, 1))).astype(np.float32),
        "dx": (n((G, D, N)) * s_d[:, None]).astype(np.float32),
        "og": (np.random.uniform(0.5, 2.0, (G, M, 1))).astype(np.float32),
        "base": (0.3 * n((G, M, N))).astype(np.float32),
    }


def reference(x, w1, w2, tp, dx, og, base):
    w1q = mxq(f64(w1), 1, "e4m3")
    xq = mxq(f64(x), 1, "e4m3")
    z1 = w1q.transpose(0, 2, 1) @ xq
    dxq = mxq(f64(dx), 1, "e4m3")
    tz1 = w1q.transpose(0, 2, 1) @ dxq
    w2q = mxq(f64(w2), 1, "e4m3")
    z2 = w2q.transpose(0, 2, 1) @ xq
    tz2 = w2q.transpose(0, 2, 1) @ dxq
    p1 = np.exp(z1 * f64(tp) - np.max(z1 * f64(tp), axis=-1, keepdims=True))
    zs = np.sum(p1, axis=-1, keepdims=True)
    xp1 = tz1 * f64(tp) * p1
    xzs = np.sum(xp1, axis=-1, keepdims=True)
    xh = ((xp1 - xzs * p1 / zs) / zs * z2 + tz2 * p1 / zs) * 512.0
    y = xh * f64(og) + f64(base)
    Y = y.reshape(G * M, N)
    words, scales = planes(Y)
    return Y, words, scales

@@ -1,0 +1,282 @@
+from contextlib import ExitStack
+
+import concourse.mybir as mybir
+
+G, D, M, N = 2, 256, 256, 512
+FLOPS = 4 * 2 * G * D * M * N
+
+F32 = mybir.dt.float32
+BF16 = mybir.dt.bfloat16
+U32 = mybir.dt.uint32
+I32 = mybir.dt.int32
+U8 = mybir.dt.uint8
+FP8X4 = mybir.dt.float8_e4m3fn_x4
+ALU = mybir.AluOpType
+ACT = mybir.ActivationFunctionType
+
+P = 128
+PACK = 4
+ROWS = D // PACK
+HALVES = M // P
+QUAD = 32
+HALF_N = N // 2
+X_ON_VECTOR = 344
+DX_ON_VECTOR = 264
+OUT_ON_VECTOR = 176
+
+
+def tile_rows_pl_tnrowsoft_kernel(tc, x, w1, w2, tp, dx, og, base, out_0, out_1, out_2):
+    nc = tc.nc
+    with ExitStack() as ctx:
+        sb = ctx.enter_context(tc.tile_pool(name="sb", bufs=1))
+        ps = ctx.enter_context(tc.psum_pool(name="ps", bufs=1))
+        ctx.enter_context(tc.manual_schedule())
+
+        def sbuf(name, shape, dtype):
+            return sb.tile(shape, dtype, name=name, align_bytes=64)
+
+        def operand(name, width):
+            return {
+                "raw": sbuf(name + "_raw", [P, PACK, width], F32),
+                "packed": sbuf(name + "_packed", [P, width, PACK], BF16),
+                "codes": sbuf(name + "_codes", [P, width], U32),
+                "scales": sbuf(name + "_scales", [P, width], U8),
+            }
+
+        def load(op, src):
+            nc.sync.dma_start(out=op["raw"][:], in_=src.rearrange("g (q j) c -> (g q) j c", j=PACK))
+
+        def interleave(copy, op, lo, hi):
+            copy(
+                out=op["packed"][:, lo:hi, :].rearrange("p (c i) j -> p c j i", i=4),
+                in_=op["raw"][:, :, lo:hi].rearrange("p j (c i) -> p c j i", i=4),
+            )
+
+        def quantize(op, lo, hi, scales, at):
+            nc.vector.quantize_mx(
+                out=op["codes"][:, lo:hi].bitcast(FP8X4),
+                scales=scales[:, at : at + hi - lo],
+                in_=op["packed"][:, lo:hi, :].rearrange("p c j -> p (c j)"),
+            )
+
+        def product(bank, w, a, g, h):
+            rows = slice(ROWS * g, ROWS * (g + 1))
+            cols = slice(P * h, P * (h + 1))
+            nc.tensor.matmul_mx(
+                out=bank[:],
+                lhsT=w["codes"][rows, cols].bitcast(FP8X4),
+                lhsT_scale=w["scales"][rows, cols],
+                rhs=a["codes"][rows, :].bitcast(FP8X4),
+                rhs_scale=a["scales"][rows, :],
+                start=True,
+                stop=True,
+            )
+
+        xo, dxo = operand("x", N), operand("dx", N)
+        w1o, w2o = operand("w1", M), operand("w2", M)
+        banks = [[ps.tile([P, N], F32, name="bank_%d_%d" % (g, b)) for b in range(4)] for g in range(G)]
+        tiles = [(g, h) for h in range(HALVES) for g in range(G)]
+
+        vec_rows = sbuf("vec_rows", [P, P], F32)
+        vec_cols = sbuf("vec_cols", [P, G, HALVES, QUAD], F32)
+        neg_tp = sbuf("neg_tp", [P, HALVES, G], F32)
+        gains = sbuf("gains", [P, HALVES, 2, G], F32)
+        coef = [sbuf("coef%d" % h, [P, 2, G], F32) for h in range(HALVES)]
+        neg_max = sbuf("neg_max", [P, HALVES, G], F32)
+        zs = [sbuf("zs%d" % h, [P, G], F32) for h in range(HALVES)]
+        inv_zs = [sbuf("inv_zs%d" % h, [P, G], F32) for h in range(HALVES)]
+        mean_tz = sbuf("mean_tz", [P, HALVES, G], F32)
+        base_sb = sbuf("base_sb", [P, G * HALVES, N], F32)
+        work = {}
+        for g, h in tiles:
+            for name in ("s", "p", "u", "z2", "t2", "t3", "t4", "y"):
+                work[name, g, h] = sbuf("%s_%d_%d" % (name, g, h), [P, N], F32)
+        res = []
+        for h in range(HALVES):
+            res.append({
+                "raw": sbuf("res_raw%d" % h, [P, PACK, HALF_N], F32),
+                "packed": sbuf("res_packed%d" % h, [P, HALF_N, PACK], BF16),
+                "codes": sbuf("res_codes%d" % h, [P, HALF_N], U32),
+            })
+        res_scales = sbuf("res_scales", [P, HALVES * HALF_N], U8)
+
+        nc.gpsimd.memset(vec_rows[:], 0.0)
+        load(xo, x)
+        for k, vec in enumerate((tp, og)):
+            nc.sync.dma_start(
+                out=vec_rows[k:P:QUAD, :].rearrange("q (t i) -> q t i", i=QUAD),
+                in_=vec.rearrange("g (h q i) o -> q (g h) (i o)", h=HALVES, i=QUAD),
+            )
+        load(w1o, w1)
+        load(dxo, dx)
+        load(w2o, w2)
+        nc.sync.dma_start(out=base_sb[:], in_=base.rearrange("g (h j) n -> j (g h) n", j=P))
+
+        vcopy, scopy = nc.vector.tensor_copy, nc.scalar.copy
+        interleave(vcopy, xo, 0, X_ON_VECTOR)
+        nc.vector.transpose(out=vec_cols[:].rearrange("p g h i -> p (g h i)"), in_=vec_rows[:])
+        tp_cols = vec_cols[:, :, :, 0].rearrange("p g h -> p h g")
+        og_cols = vec_cols[:, :, :, 1].rearrange("p g h -> p h g")
+        nc.vector.tensor_scalar(out=neg_tp[:], in0=tp_cols, scalar1=-1.0, scalar2=None, op0=ALU.mult)
+        nc.vector.tensor_scalar(out=gains[:, :, 0, :], in0=og_cols, scalar1=float(N), scalar2=None, op0=ALU.mult)
+        nc.vector.scalar_tensor_tensor(
+            out=gains[:, :, 1, :], in0=og_cols, scalar=float(N), in1=tp_cols, op0=ALU.mult, op1=ALU.mult
+        )
+
+        def row_max(g, h):
+            nc.vector.tensor_scalar(
+                out=work["s", g, h][:], in0=banks[g][h][:], scalar1=neg_tp[:, h, g : g + 1], scalar2=None,
+                op0=ALU.mult, op1=ALU.min, accum_out=neg_max[:, h, g : g + 1],
+            )
+
+        def exponential(g, h):
+            nc.scalar.activation(
+                out=work["p", g, h][:], in_=work["s", g, h][:], func=ACT.Exp, scale=-1.0,
+                bias=neg_max[:, h, g : g + 1], accum_out=zs[h][:, g : g + 1],
+            )
+
+        def reciprocal(h):
+            nc.vector.reciprocal(out=inv_zs[h][:], in_=zs[h][:])
+
+        def coefficients(h):
+            nc.vector.tensor_tensor(
+                out=coef[h][:], in0=gains[:, h, :, :], in1=inv_zs[h][:].unsqueeze(1).to_broadcast([P, 2, G]),
+                op=ALU.mult,
+            )
+
+        def mean(g, h):
+            nc.vector.scalar_tensor_tensor(
+                out=work["u", g, h][:], in0=banks[g][2 + h][:], scalar=inv_zs[h][:, g : g + 1],
+                in1=work["p", g, h][:], op0=ALU.mult, op1=ALU.mult, accum_out=mean_tz[:, h, g : g + 1],
+            )
+
+        def scale_z2(g, h):
+            nc.scalar.activation(
+                out=work["z2", g, h][:], in_=banks[g][0][:], func=ACT.Copy, scale=coef[h][:, 1, g : g + 1]
+            )
+
+        def step2(g, h):
+            nc.vector.scalar_tensor_tensor(
+                out=work["t2", g, h][:], in0=banks[g][2 + h][:], scalar=mean_tz[:, h, g : g + 1],
+                in1=work["z2", g, h][:], op0=ALU.subtract, op1=ALU.mult,
+            )
+
+        def step3(g, h):
+            nc.vector.scalar_tensor_tensor(
+                out=work["t3", g, h][:], in0=banks[g][1 + h][:], scalar=coef[h][:, 0, g : g + 1],
+                in1=work["t2", g, h][:], op0=ALU.mult, op1=ALU.add,
+            )
+
+        def step4(engine, g, h):
+            engine.tensor_tensor(
+                out=work["t4", g, h][:], in0=work["t3", g, h][:], in1=work["p", g, h][:], op=ALU.mult
+            )
+
+        def step5(engine, g, h):
+            engine.tensor_tensor(
+                out=work["y", g, h][:], in0=work["t4", g, h][:], in1=base_sb[:, HALVES * g + h, :], op=ALU.add
+            )
+
+        def hand_out(queues, g, h):
+            y = work["y", g, h]
+            for c in range(2):
+                at = 2 * QUAD * c + QUAD * g
+                queues[c].dma_start(
+                    out=res[h]["raw"][at : at + QUAD, :, :], in_=y[:, HALF_N * c : HALF_N * (c + 1)]
+                )
+            row = M * g + P * h
+            nc.sync.dma_start(out=out_0[row : row + P, :], in_=y[:])
+
+        words_out = out_1.rearrange("v p n u -> (v p) (n u)").bitcast(I32)
+        scales_out = out_2.rearrange("v f n -> (v f) n").bitcast(I32).rearrange(
+            "(g h r) (c w) -> c g r h w", g=G, h=HALVES, c=2
+        )
+
+        def store_words(queues, h):
+            for c in range(2):
+                for g in range(G):
+                    at = 2 * QUAD * c + QUAD * g
+                    row = ROWS * g + QUAD * h
+                    queues[g].dma_start(
+                        out=words_out[row : row + QUAD, HALF_N * c : HALF_N * (c + 1)],
+                        in_=res[h]["codes"][at : at + QUAD, :].bitcast(I32),
+                    )
+
+        def store_scales(queues):
+            for c in range(2):
+                for g in range(G):
+                    at = 2 * QUAD * c + QUAD * g
+                    queues[g].dma_start(
+                        out=scales_out[c, g],
+                        in_=res_scales[at : at + 4, :].bitcast(I32).rearrange("r (h w) -> r h w", h=HALVES),
+                    )
+
+        interleave(scopy, xo, X_ON_VECTOR, N)
+        interleave(scopy, w1o, 0, P)
+        quantize(xo, 0, N, xo["scales"], 0)
+        interleave(vcopy, w1o, P, M)
+        quantize(w1o, 0, P, w1o["scales"], 0)
+        quantize(w1o, P, M, w1o["scales"], P)
+        for g, h in tiles:
+            product(banks[g][h], w1o, xo, g, h)
+
+        interleave(scopy, dxo, DX_ON_VECTOR, N)
+        row_max(0, 0)
+        row_max(1, 0)
+        exponential(0, 0)
+        exponential(1, 0)
+        interleave(vcopy, dxo, 0, DX_ON_VECTOR)
+        row_max(0, 1)
+        quantize(dxo, 0, N, dxo["scales"], 0)
+        for g, h in tiles:
+            product(banks[g][2 + h], w1o, dxo, g, h)
+        interleave(scopy, w2o, 0, P)
+        reciprocal(0)
+        row_max(1, 1)
+        quantize(w2o, 0, P, w2o["scales"], 0)
+        coefficients(0)
+        for g in range(G):
+            product(banks[g][0], w2o, xo, g, 0)
+        for g in range(G):
+            product(banks[g][1], w2o, dxo, g, 0)
+        exponential(0, 1)
+        interleave(scopy, w2o, P, M)
+        mean(0, 0)
+        mean(1, 0)
+        scale_z2(0, 0)
+        scale_z2(1, 0)
+        exponential(1, 1)
+        quantize(w2o, P, M, w2o["scales"], P)
+        for g in range(G):
+            product(banks[g][0], w2o, xo, g, 1)
+        step2(0, 0)
+        reciprocal(1)
+        step2(1, 0)
+        coefficients(1)
+        for g in range(G):
+            product(banks[g][2], w2o, dxo, g, 1)
+        for g in range(G):
+            step3(g, 0)
+        for g in range(G):
+            scale_z2(g, 1)
+        for g in range(G):
+            step4(nc.gpsimd, g, 0)
+            step5(nc.gpsimd, g, 0)
+            hand_out((nc.sync, nc.sync), g, 0)
+        for step in (mean, step2, step3):
+            for g in range(G):
+                step(g, 1)
+        for g in range(G):
+            step4(nc.vector, g, 1)
+        for g in range(G):
+            step5(nc.vector, g, 1)
+            hand_out((nc.sync, nc.scalar), g, 1)
+
+        interleave(vcopy, res[0], 0, HALF_N)
+        quantize(res[0], 0, HALF_N, res_scales, 0)
+        store_words((nc.sync, nc.scalar), 0)
+        interleave(vcopy, res[1], 0, OUT_ON_VECTOR)
+        interleave(scopy, res[1], OUT_ON_VECTOR, HALF_N)
+        quantize(res[1], 0, HALF_N, res_scales, HALF_N)
+        store_words((nc.sync, nc.scalar), 1)
+        store_scales((nc.sync, nc.scalar))

@@ -86,14 +86,20 @@ def tile_rows_pl_tnrowsoft_kernel(tc, x, w1, w2, tp, dx, og, base, out_0, out_1,
         zs = [sbuf("zs%d" % h, [P, G], F32) for h in range(HALVES)]
         inv_zs = [sbuf("inv_zs%d" % h, [P, G], F32) for h in range(HALVES)]
         mean_tz = sbuf("mean_tz", [P, HALVES, G], F32)
-        base_sb = sbuf("base_sb", [P, G * HALVES, N], F32)
+        base_sb = sbuf("base_sb", [P, PACK, N], F32)
+        p_rows = sbuf("p_rows", [P, PACK, N], F32)
         work = {}
         for g, h in tiles:
-            for name in ("s", "p", "u", "z2", "t2", "t3", "t4", "y"):
+            for name in ("s", "p", "u", "z2"):
                 work[name, g, h] = sbuf("%s_%d_%d" % (name, g, h), [P, N], F32)
+            for c in range(2):
+                for name in ("t2", "t3"):
+                    work[name, g, h, c] = sbuf("%s_%d_%d_%d" % (name, g, h, c), [P, HALF_N], F32)
         res = []
-        for h in range(HALVES):
+        for h in range(2):
             res.append({
+                "t3": sbuf("res_t3%d" % h, [P, PACK, HALF_N], F32),
+                "t4": sbuf("res_t4%d" % h, [P, PACK, HALF_N], F32),
                 "raw": sbuf("res_raw%d" % h, [P, PACK, HALF_N], F32),
                 "packed": sbuf("res_packed%d" % h, [P, HALF_N, PACK], BF16),
                 "codes": sbuf("res_codes%d" % h, [P, HALF_N], U32),
@@ -102,26 +108,27 @@ def tile_rows_pl_tnrowsoft_kernel(tc, x, w1, w2, tp, dx, og, base, out_0, out_1,
 
         nc.gpsimd.memset(vec_rows[:], 0.0)
         load(xo, x)
+        load(w1o, w1)
         for k, vec in enumerate((tp, og)):
             nc.sync.dma_start(
                 out=vec_rows[k:P:QUAD, :].rearrange("q (t i) -> q t i", i=QUAD),
                 in_=vec.rearrange("g (h q i) o -> q (g h) (i o)", h=HALVES, i=QUAD),
             )
-        load(w1o, w1)
         load(dxo, dx)
         load(w2o, w2)
-        nc.sync.dma_start(out=base_sb[:], in_=base.rearrange("g (h j) n -> j (g h) n", j=P))
+        nc.sync.dma_start(out=base_sb[:], in_=base.rearrange("g (q t) n -> (g q) t n", t=PACK))
 
         vcopy, scopy = nc.vector.tensor_copy, nc.scalar.copy
-        interleave(vcopy, xo, 0, X_ON_VECTOR)
-        nc.vector.transpose(out=vec_cols[:].rearrange("p g h i -> p (g h i)"), in_=vec_rows[:])
-        tp_cols = vec_cols[:, :, :, 0].rearrange("p g h -> p h g")
-        og_cols = vec_cols[:, :, :, 1].rearrange("p g h -> p h g")
-        nc.vector.tensor_scalar(out=neg_tp[:], in0=tp_cols, scalar1=-1.0, scalar2=None, op0=ALU.mult)
-        nc.vector.tensor_scalar(out=gains[:, :, 0, :], in0=og_cols, scalar1=float(N), scalar2=None, op0=ALU.mult)
-        nc.vector.scalar_tensor_tensor(
-            out=gains[:, :, 1, :], in0=og_cols, scalar=float(N), in1=tp_cols, op0=ALU.mult, op1=ALU.mult
-        )
+
+        def row_constants():
+            nc.vector.transpose(out=vec_cols[:].rearrange("p g h i -> p (g h i)"), in_=vec_rows[:])
+            tp_cols = vec_cols[:, :, :, 0].rearrange("p g h -> p h g")
+            og_cols = vec_cols[:, :, :, 1].rearrange("p g h -> p h g")
+            nc.vector.tensor_scalar(out=neg_tp[:], in0=tp_cols, scalar1=-1.0, scalar2=None, op0=ALU.mult)
+            nc.vector.tensor_scalar(out=gains[:, :, 0, :], in0=og_cols, scalar1=float(N), scalar2=None, op0=ALU.mult)
+            nc.vector.scalar_tensor_tensor(
+                out=gains[:, :, 1, :], in0=og_cols, scalar=float(N), in1=tp_cols, op0=ALU.mult, op1=ALU.mult
+            )
 
         def row_max(g, h):
             nc.vector.tensor_scalar(
@@ -152,131 +159,132 @@ def tile_rows_pl_tnrowsoft_kernel(tc, x, w1, w2, tp, dx, og, base, out_0, out_1,
 
         def scale_z2(g, h):
             nc.scalar.activation(
-                out=work["z2", g, h][:], in_=banks[g][0][:], func=ACT.Copy, scale=coef[h][:, 1, g : g + 1]
+                out=work["z2", g, h][:], in_=banks[g][h][:], func=ACT.Copy, scale=coef[h][:, 1, g : g + 1]
             )
 
-        def step2(g, h):
+        def step2(g, h, c):
+            cols = slice(HALF_N * c, HALF_N * (c + 1))
             nc.vector.scalar_tensor_tensor(
-                out=work["t2", g, h][:], in0=banks[g][2 + h][:], scalar=mean_tz[:, h, g : g + 1],
-                in1=work["z2", g, h][:], op0=ALU.subtract, op1=ALU.mult,
+                out=work["t2", g, h, c][:], in0=banks[g][2 + h][:, cols], scalar=mean_tz[:, h, g : g + 1],
+                in1=work["z2", g, h][:, cols], op0=ALU.subtract, op1=ALU.mult,
             )
 
-        def step3(g, h):
+        def step3(g, h, c):
+            cols = slice(HALF_N * c, HALF_N * (c + 1))
             nc.vector.scalar_tensor_tensor(
-                out=work["t3", g, h][:], in0=banks[g][1 + h][:], scalar=coef[h][:, 0, g : g + 1],
-                in1=work["t2", g, h][:], op0=ALU.mult, op1=ALU.add,
+                out=work["t3", g, h, c][:], in0=banks[g][h][:, cols], scalar=coef[h][:, 0, g : g + 1],
+                in1=work["t2", g, h, c][:], op0=ALU.mult, op1=ALU.add,
             )
 
-        def step4(engine, g, h):
-            engine.tensor_tensor(
-                out=work["t4", g, h][:], in0=work["t3", g, h][:], in1=work["p", g, h][:], op=ALU.mult
+        def regroup(queue, dst, src, g, h):
+            at = ROWS * g + QUAD * h
+            queue.dma_start(out=dst[at : at + QUAD, :, :], in_=src[:])
+
+        def weigh(c, lo, hi):
+            nc.vector.tensor_tensor(
+                out=res[c]["t4"][:, :, lo:hi], in0=res[c]["t3"][:, :, lo:hi],
+                in1=p_rows[:, :, HALF_N * c + lo : HALF_N * c + hi], op=ALU.mult,
             )
 
-        def step5(engine, g, h):
-            engine.tensor_tensor(
-                out=work["y", g, h][:], in0=work["t4", g, h][:], in1=base_sb[:, HALVES * g + h, :], op=ALU.add
+        def add_base(c, lo, hi):
+            nc.vector.tensor_tensor(
+                out=res[c]["raw"][:, :, lo:hi], in0=res[c]["t4"][:, :, lo:hi],
+                in1=base_sb[:, :, HALF_N * c + lo : HALF_N * c + hi], op=ALU.add,
             )
 
-        def hand_out(queues, g, h):
-            y = work["y", g, h]
-            for c in range(2):
-                at = 2 * QUAD * c + QUAD * g
-                queues[c].dma_start(
-                    out=res[h]["raw"][at : at + QUAD, :, :], in_=y[:, HALF_N * c : HALF_N * (c + 1)]
-                )
-            row = M * g + P * h
-            nc.sync.dma_start(out=out_0[row : row + P, :], in_=y[:])
+        def store_result(c):
+            cols = slice(HALF_N * c, HALF_N * (c + 1))
+            nc.sync.dma_start(out=out_0.rearrange("(p t) n -> p t n", t=PACK)[:, :, cols], in_=res[c]["raw"][:])
 
         words_out = out_1.rearrange("v p n u -> (v p) (n u)").bitcast(I32)
-        scales_out = out_2.rearrange("v f n -> (v f) n").bitcast(I32).rearrange(
-            "(g h r) (c w) -> c g r h w", g=G, h=HALVES, c=2
-        )
+        scales_out = out_2.rearrange("v f n -> (v f) n").bitcast(I32)
 
-        def store_words(queues, h):
-            for c in range(2):
-                for g in range(G):
-                    at = 2 * QUAD * c + QUAD * g
-                    row = ROWS * g + QUAD * h
-                    queues[g].dma_start(
-                        out=words_out[row : row + QUAD, HALF_N * c : HALF_N * (c + 1)],
-                        in_=res[h]["codes"][at : at + QUAD, :].bitcast(I32),
-                    )
+        def store_words(c):
+            nc.sync.dma_start(
+                out=words_out[:, HALF_N * c : HALF_N * (c + 1)], in_=res[c]["codes"][:].bitcast(I32)
+            )
 
         def store_scales(queues):
-            for c in range(2):
-                for g in range(G):
-                    at = 2 * QUAD * c + QUAD * g
-                    queues[g].dma_start(
-                        out=scales_out[c, g],
-                        in_=res_scales[at : at + 4, :].bitcast(I32).rearrange("r (h w) -> r h w", h=HALVES),
-                    )
+            for q in range(P // QUAD):
+                queues[q % 2].dma_start(
+                    out=scales_out[4 * q : 4 * q + 4, :], in_=res_scales[QUAD * q : QUAD * q + 4, :].bitcast(I32)
+                )
 
+        interleave(vcopy, xo, 0, X_ON_VECTOR)
         interleave(scopy, xo, X_ON_VECTOR, N)
         interleave(scopy, w1o, 0, P)
+        interleave(scopy, w1o, P, M)
         quantize(xo, 0, N, xo["scales"], 0)
-        interleave(vcopy, w1o, P, M)
         quantize(w1o, 0, P, w1o["scales"], 0)
+        for g in range(G):
+            product(banks[g][0], w1o, xo, g, 0)
+        row_constants()
         quantize(w1o, P, M, w1o["scales"], P)
-        for g, h in tiles:
-            product(banks[g][h], w1o, xo, g, h)
+        for g in range(G):
+            product(banks[g][1], w1o, xo, g, 1)
 
         interleave(scopy, dxo, DX_ON_VECTOR, N)
-        row_max(0, 0)
-        row_max(1, 0)
-        exponential(0, 0)
-        exponential(1, 0)
+        for g in range(G):
+            row_max(g, 0)
+            exponential(g, 0)
+            regroup(nc.sync, p_rows, work["p", g, 0], g, 0)
         interleave(vcopy, dxo, 0, DX_ON_VECTOR)
         row_max(0, 1)
         quantize(dxo, 0, N, dxo["scales"], 0)
-        for g, h in tiles:
-            product(banks[g][2 + h], w1o, dxo, g, h)
+        for g in range(G):
+            product(banks[g][2], w1o, dxo, g, 0)
         interleave(scopy, w2o, 0, P)
-        reciprocal(0)
         row_max(1, 1)
+        reciprocal(0)
         quantize(w2o, 0, P, w2o["scales"], 0)
         coefficients(0)
         for g in range(G):
+            product(banks[g][3], w1o, dxo, g, 1)
+        for g in range(G):
             product(banks[g][0], w2o, xo, g, 0)
         for g in range(G):
-            product(banks[g][1], w2o, dxo, g, 0)
-        exponential(0, 1)
+            exponential(g, 1)
+            regroup(nc.sync, p_rows, work["p", g, 1], g, 1)
         interleave(scopy, w2o, P, M)
-        mean(0, 0)
-        mean(1, 0)
-        scale_z2(0, 0)
-        scale_z2(1, 0)
-        exponential(1, 1)
-        quantize(w2o, P, M, w2o["scales"], P)
         for g in range(G):
-            product(banks[g][0], w2o, xo, g, 1)
-        step2(0, 0)
+            mean(g, 0)
+            scale_z2(g, 0)
         reciprocal(1)
-        step2(1, 0)
+        quantize(w2o, P, M, w2o["scales"], P)
         coefficients(1)
         for g in range(G):
-            product(banks[g][2], w2o, dxo, g, 1)
+            product(banks[g][1], w2o, xo, g, 1)
         for g in range(G):
-            step3(g, 0)
+            product(banks[g][0], w2o, dxo, g, 0)
         for g in range(G):
+            mean(g, 1)
             scale_z2(g, 1)
         for g in range(G):
-            step4(nc.gpsimd, g, 0)
-            step5(nc.gpsimd, g, 0)
-            hand_out((nc.sync, nc.sync), g, 0)
-        for step in (mean, step2, step3):
-            for g in range(G):
-                step(g, 1)
-        for g in range(G):
-            step4(nc.vector, g, 1)
-        for g in range(G):
-            step5(nc.vector, g, 1)
-            hand_out((nc.sync, nc.scalar), g, 1)
+            product(banks[g][1], w2o, dxo, g, 1)
 
-        interleave(vcopy, res[0], 0, HALF_N)
+        queues = (nc.sync, nc.scalar)
+        for c in range(2):
+            for g, h in tiles:
+                step2(g, h, c)
+            for g, h in tiles:
+                step3(g, h, c)
+                regroup(queues[g], res[c]["t3"], work["t3", g, h, c], g, h)
+
+        mid = HALF_N // 2
+        weigh(0, 0, mid)
+        weigh(0, mid, HALF_N)
+        add_base(0, 0, mid)
+        add_base(0, mid, HALF_N)
+        store_result(0)
+        interleave(scopy, res[0], 0, HALF_N)
+        weigh(1, 0, HALF_N)
         quantize(res[0], 0, HALF_N, res_scales, 0)
-        store_words((nc.sync, nc.scalar), 0)
-        interleave(vcopy, res[1], 0, OUT_ON_VECTOR)
-        interleave(scopy, res[1], OUT_ON_VECTOR, HALF_N)
+        store_words(0)
+        add_base(1, 0, mid)
+        interleave(scopy, res[1], 0, mid)
+        add_base(1, mid, HALF_N)
+        store_result(1)
+        interleave(vcopy, res[1], mid, HALF_N)
         quantize(res[1], 0, HALF_N, res_scales, HALF_N)
-        store_words((nc.sync, nc.scalar), 1)
-        store_scales((nc.sync, nc.scalar))
+        store_words(1)
+        store_scales((nc.scalar, nc.sync))

@@ -21,8 +21,8 @@ HALVES = M // P
 QUAD = 32
 HALF_N = N // 2
 X_ON_VECTOR = 344
-DX_ON_VECTOR = 264
-OUT_ON_VECTOR = 176
+DX_ON_GPSIMD = 240
+OUT_ON_VECTOR = 88
 
 
 def tile_rows_pl_tnrowsoft_kernel(tc, x, w1, w2, tp, dx, og, base, out_0, out_1, out_2):
@@ -48,8 +48,8 @@ def tile_rows_pl_tnrowsoft_kernel(tc, x, w1, w2, tp, dx, og, base, out_0, out_1,
 
         def interleave(copy, op, lo, hi):
             copy(
-                out=op["packed"][:, lo:hi, :].rearrange("p (c i) j -> p c j i", i=4),
-                in_=op["raw"][:, :, lo:hi].rearrange("p j (c i) -> p c j i", i=4),
+                out=op["packed"][:, lo:hi, :].rearrange("p (c i) j -> p c j i", i=2),
+                in_=op["raw"][:, :, lo:hi].rearrange("p j (c i) -> p c j i", i=2),
             )
 
         def quantize(op, lo, hi, scales, at):
@@ -90,11 +90,10 @@ def tile_rows_pl_tnrowsoft_kernel(tc, x, w1, w2, tp, dx, og, base, out_0, out_1,
         p_rows = sbuf("p_rows", [P, PACK, N], F32)
         work = {}
         for g, h in tiles:
-            for name in ("s", "p", "u", "z2"):
+            for name in ("s", "p", "u", "z2", "t2"):
                 work[name, g, h] = sbuf("%s_%d_%d" % (name, g, h), [P, N], F32)
             for c in range(2):
-                for name in ("t2", "t3"):
-                    work[name, g, h, c] = sbuf("%s_%d_%d_%d" % (name, g, h, c), [P, HALF_N], F32)
+                work["t3", g, h, c] = sbuf("t3_%d_%d_%d" % (g, h, c), [P, HALF_N], F32)
         res = []
         for h in range(2):
             res.append({
@@ -114,11 +113,17 @@ def tile_rows_pl_tnrowsoft_kernel(tc, x, w1, w2, tp, dx, og, base, out_0, out_1,
                 out=vec_rows[k:P:QUAD, :].rearrange("q (t i) -> q t i", i=QUAD),
                 in_=vec.rearrange("g (h q i) o -> q (g h) (i o)", h=HALVES, i=QUAD),
             )
-        load(dxo, dx)
         load(w2o, w2)
+        load(dxo, dx)
         nc.sync.dma_start(out=base_sb[:], in_=base.rearrange("g (q t) n -> (g q) t n", t=PACK))
 
         vcopy, scopy = nc.vector.tensor_copy, nc.scalar.copy
+
+        def gcopy(out, in_):
+            nc.gpsimd.tensor_scalar(out=out, in0=in_, scalar1=1.0, scalar2=0.0, op0=ALU.mult, op1=ALU.add)
+
+        def interleave_gpsimd(op, lo, hi):
+            gcopy(op["packed"][:, lo:hi, :], op["raw"][:, :, lo:hi].rearrange("p j c -> p c j"))
 
         def row_constants():
             nc.vector.transpose(out=vec_cols[:].rearrange("p g h i -> p (g h i)"), in_=vec_rows[:])
@@ -151,29 +156,29 @@ def tile_rows_pl_tnrowsoft_kernel(tc, x, w1, w2, tp, dx, og, base, out_0, out_1,
                 op=ALU.mult,
             )
 
-        def mean(g, h):
+        def mean(g, h, b=0):
             nc.vector.scalar_tensor_tensor(
-                out=work["u", g, h][:], in0=banks[g][2 + h][:], scalar=inv_zs[h][:, g : g + 1],
+                out=work["u", g, h][:], in0=banks[g][b + h][:], scalar=inv_zs[h][:, g : g + 1],
                 in1=work["p", g, h][:], op0=ALU.mult, op1=ALU.mult, accum_out=mean_tz[:, h, g : g + 1],
             )
 
         def scale_z2(g, h):
             nc.scalar.activation(
-                out=work["z2", g, h][:], in_=banks[g][h][:], func=ACT.Copy, scale=coef[h][:, 1, g : g + 1]
+                out=work["z2", g, h][:], in_=banks[g][2 + h][:], func=ACT.Copy, scale=coef[h][:, 1, g : g + 1]
             )
 
-        def step2(g, h, c):
-            cols = slice(HALF_N * c, HALF_N * (c + 1))
+        def step2(g, h, lo, hi):
+            cols = slice(lo, hi)
             nc.vector.scalar_tensor_tensor(
-                out=work["t2", g, h, c][:], in0=banks[g][2 + h][:, cols], scalar=mean_tz[:, h, g : g + 1],
+                out=work["t2", g, h][:, cols], in0=banks[g][h][:, cols], scalar=mean_tz[:, h, g : g + 1],
                 in1=work["z2", g, h][:, cols], op0=ALU.subtract, op1=ALU.mult,
             )
 
         def step3(g, h, c):
             cols = slice(HALF_N * c, HALF_N * (c + 1))
             nc.vector.scalar_tensor_tensor(
-                out=work["t3", g, h, c][:], in0=banks[g][h][:, cols], scalar=coef[h][:, 0, g : g + 1],
-                in1=work["t2", g, h, c][:], op0=ALU.mult, op1=ALU.add,
+                out=work["t3", g, h, c][:], in0=banks[g][2 + h][:, cols], scalar=coef[h][:, 0, g : g + 1],
+                in1=work["t2", g, h][:, cols], op0=ALU.mult, op1=ALU.add,
             )
 
         def regroup(queue, dst, src, g, h):
@@ -192,16 +197,18 @@ def tile_rows_pl_tnrowsoft_kernel(tc, x, w1, w2, tp, dx, og, base, out_0, out_1,
                 in1=base_sb[:, :, HALF_N * c + lo : HALF_N * c + hi], op=ALU.add,
             )
 
-        def store_result(c):
-            cols = slice(HALF_N * c, HALF_N * (c + 1))
-            nc.sync.dma_start(out=out_0.rearrange("(p t) n -> p t n", t=PACK)[:, :, cols], in_=res[c]["raw"][:])
+        def store_result(c, lo, hi):
+            cols = slice(HALF_N * c + lo, HALF_N * c + hi)
+            nc.sync.dma_start(
+                out=out_0.rearrange("(p t) n -> p t n", t=PACK)[:, :, cols], in_=res[c]["raw"][:, :, lo:hi]
+            )
 
         words_out = out_1.rearrange("v p n u -> (v p) (n u)").bitcast(I32)
         scales_out = out_2.rearrange("v f n -> (v f) n").bitcast(I32)
 
-        def store_words(c):
-            nc.sync.dma_start(
-                out=words_out[:, HALF_N * c : HALF_N * (c + 1)], in_=res[c]["codes"][:].bitcast(I32)
+        def store_words(queue, c, lo, hi):
+            queue.dma_start(
+                out=words_out[:, HALF_N * c + lo : HALF_N * c + hi], in_=res[c]["codes"][:, lo:hi].bitcast(I32)
             )
 
         def store_scales(queues):
@@ -210,11 +217,13 @@ def tile_rows_pl_tnrowsoft_kernel(tc, x, w1, w2, tp, dx, og, base, out_0, out_1,
                     out=scales_out[4 * q : 4 * q + 4, :], in_=res_scales[QUAD * q : QUAD * q + 4, :].bitcast(I32)
                 )
 
-        interleave(vcopy, xo, 0, X_ON_VECTOR)
-        interleave(scopy, xo, X_ON_VECTOR, N)
-        interleave(scopy, w1o, 0, P)
+        interleave(vcopy, xo, 0, 288)
+        interleave(scopy, xo, 288, N)
+        quantize(xo, 0, HALF_N, xo["scales"], 0)
+        interleave(vcopy, w1o, 0, 64)
+        interleave(scopy, w1o, 64, P)
         interleave(scopy, w1o, P, M)
-        quantize(xo, 0, N, xo["scales"], 0)
+        quantize(xo, HALF_N, N, xo["scales"], HALF_N)
         quantize(w1o, 0, P, w1o["scales"], 0)
         for g in range(G):
             product(banks[g][0], w1o, xo, g, 0)
@@ -223,49 +232,45 @@ def tile_rows_pl_tnrowsoft_kernel(tc, x, w1, w2, tp, dx, og, base, out_0, out_1,
         for g in range(G):
             product(banks[g][1], w1o, xo, g, 1)
 
-        interleave(scopy, dxo, DX_ON_VECTOR, N)
-        for g in range(G):
-            row_max(g, 0)
-            exponential(g, 0)
-            regroup(nc.sync, p_rows, work["p", g, 0], g, 0)
-        interleave(vcopy, dxo, 0, DX_ON_VECTOR)
+        interleave(scopy, w2o, 0, M)
+        row_max(0, 0)
+        row_max(1, 0)
+        quantize(w2o, 0, M, w2o["scales"], 0)
+        for g, h in tiles:
+            product(banks[g][2 + h], w2o, xo, g, h)
+        exponential(0, 0)
+        regroup(nc.sync, p_rows, work["p", 0, 0], 0, 0)
         row_max(0, 1)
+        interleave(vcopy, dxo, 0, 288)
+        interleave(scopy, dxo, 288, N)
+        exponential(1, 0)
         quantize(dxo, 0, N, dxo["scales"], 0)
-        for g in range(G):
-            product(banks[g][2], w1o, dxo, g, 0)
-        interleave(scopy, w2o, 0, P)
         row_max(1, 1)
+        for g, h in tiles:
+            product(banks[g][h], w1o, dxo, g, h)
         reciprocal(0)
-        quantize(w2o, 0, P, w2o["scales"], 0)
+        exponential(0, 1)
+        regroup(nc.scalar, p_rows, work["p", 1, 0], 1, 0)
+        regroup(nc.sync, p_rows, work["p", 0, 1], 0, 1)
+        exponential(1, 1)
         coefficients(0)
-        for g in range(G):
-            product(banks[g][3], w1o, dxo, g, 1)
-        for g in range(G):
-            product(banks[g][0], w2o, xo, g, 0)
-        for g in range(G):
-            exponential(g, 1)
-            regroup(nc.sync, p_rows, work["p", g, 1], g, 1)
-        interleave(scopy, w2o, P, M)
-        for g in range(G):
-            mean(g, 0)
-            scale_z2(g, 0)
+        mean(0, 0)
         reciprocal(1)
-        quantize(w2o, P, M, w2o["scales"], P)
+        mean(1, 0)
         coefficients(1)
         for g in range(G):
-            product(banks[g][1], w2o, xo, g, 1)
-        for g in range(G):
-            product(banks[g][0], w2o, dxo, g, 0)
+            scale_z2(g, 0)
+        regroup(nc.scalar, p_rows, work["p", 1, 1], 1, 1)
         for g in range(G):
             mean(g, 1)
             scale_z2(g, 1)
-        for g in range(G):
-            product(banks[g][1], w2o, dxo, g, 1)
+        for g, h in tiles:
+            product(banks[g][2 + h], w2o, dxo, g, h)
 
         queues = (nc.sync, nc.scalar)
         for c in range(2):
             for g, h in tiles:
-                step2(g, h, c)
+                step2(g, h, HALF_N * c, HALF_N * (c + 1))
             for g, h in tiles:
                 step3(g, h, c)
                 regroup(queues[g], res[c]["t3"], work["t3", g, h, c], g, h)
@@ -274,17 +279,24 @@ def tile_rows_pl_tnrowsoft_kernel(tc, x, w1, w2, tp, dx, og, base, out_0, out_1,
         weigh(0, 0, mid)
         weigh(0, mid, HALF_N)
         add_base(0, 0, mid)
+        interleave(scopy, res[0], 0, mid)
         add_base(0, mid, HALF_N)
-        store_result(0)
-        interleave(scopy, res[0], 0, HALF_N)
-        weigh(1, 0, HALF_N)
-        quantize(res[0], 0, HALF_N, res_scales, 0)
-        store_words(0)
+        store_result(0, 0, HALF_N)
+        interleave(scopy, res[0], mid, HALF_N)
+        weigh(1, 0, mid)
+        quantize(res[0], 0, mid, res_scales, 0)
         add_base(1, 0, mid)
+        store_result(1, 0, mid)
         interleave(scopy, res[1], 0, mid)
+        weigh(1, mid, HALF_N)
+        quantize(res[0], mid, HALF_N, res_scales, mid)
+        store_words(nc.sync, 0, 0, HALF_N)
         add_base(1, mid, HALF_N)
-        store_result(1)
-        interleave(vcopy, res[1], mid, HALF_N)
-        quantize(res[1], 0, HALF_N, res_scales, HALF_N)
-        store_words(1)
-        store_scales((nc.scalar, nc.sync))
+        store_result(1, mid, HALF_N)
+        quantize(res[1], 0, mid, res_scales, HALF_N)
+        interleave(vcopy, res[1], mid, mid + OUT_ON_VECTOR)
+        interleave(scopy, res[1], mid + OUT_ON_VECTOR, HALF_N)
+        store_words(nc.scalar, 1, 0, mid)
+        quantize(res[1], mid, HALF_N, res_scales, HALF_N + mid)
+        store_words(nc.scalar, 1, mid, HALF_N)
+        store_scales((nc.sync, nc.scalar))

@@ -185,22 +185,25 @@ def tile_rows_pl_tnrowsoft_kernel(tc, x, w1, w2, tp, dx, og, base, out_0, out_1,
             at = ROWS * g + QUAD * h
             queue.dma_start(out=dst[at : at + QUAD, :, :], in_=src[:])
 
-        def weigh(c, lo, hi):
+        def weigh(c, pair):
+            places = slice(2 * pair, 2 * pair + 2)
             nc.vector.tensor_tensor(
-                out=res[c]["t4"][:, :, lo:hi], in0=res[c]["t3"][:, :, lo:hi],
-                in1=p_rows[:, :, HALF_N * c + lo : HALF_N * c + hi], op=ALU.mult,
+                out=res[c]["t4"][:, places, :], in0=res[c]["t3"][:, places, :],
+                in1=p_rows[:, places, HALF_N * c : HALF_N * (c + 1)], op=ALU.mult,
             )
 
-        def add_base(c, lo, hi):
+        def add_base(c, pair, lo, hi):
+            places = slice(2 * pair, 2 * pair + 2)
             nc.vector.tensor_tensor(
-                out=res[c]["raw"][:, :, lo:hi], in0=res[c]["t4"][:, :, lo:hi],
-                in1=base_sb[:, :, HALF_N * c + lo : HALF_N * c + hi], op=ALU.add,
+                out=res[c]["raw"][:, places, lo:hi], in0=res[c]["t4"][:, places, lo:hi],
+                in1=base_sb[:, places, HALF_N * c + lo : HALF_N * c + hi], op=ALU.add,
             )
 
-        def store_result(c, lo, hi):
-            cols = slice(HALF_N * c + lo, HALF_N * c + hi)
+        def store_result(c, pair):
+            cols = slice(HALF_N * c, HALF_N * (c + 1))
+            places = slice(2 * pair, 2 * pair + 2)
             nc.sync.dma_start(
-                out=out_0.rearrange("(p t) n -> p t n", t=PACK)[:, :, cols], in_=res[c]["raw"][:, :, lo:hi]
+                out=out_0.rearrange("(p t) n -> p t n", t=PACK)[:, places, cols], in_=res[c]["raw"][:, places, :]
             )
 
         words_out = out_1.rearrange("v p n u -> (v p) (n u)").bitcast(I32)
@@ -276,27 +279,23 @@ def tile_rows_pl_tnrowsoft_kernel(tc, x, w1, w2, tp, dx, og, base, out_0, out_1,
                 regroup(queues[g], res[c]["t3"], work["t3", g, h, c], g, h)
 
         mid = HALF_N // 2
-        weigh(0, 0, mid)
-        weigh(0, mid, HALF_N)
-        add_base(0, 0, mid)
-        interleave(scopy, res[0], 0, mid)
-        add_base(0, mid, HALF_N)
-        store_result(0, 0, HALF_N)
-        interleave(scopy, res[0], mid, HALF_N)
-        weigh(1, 0, mid)
-        quantize(res[0], 0, mid, res_scales, 0)
-        add_base(1, 0, mid)
-        store_result(1, 0, mid)
+        for pair in range(2):
+            weigh(0, pair)
+        for pair in range(2):
+            add_base(0, pair, 0, HALF_N)
+            store_result(0, pair)
+        interleave(scopy, res[0], 0, HALF_N)
+        for pair in range(2):
+            weigh(1, pair)
+        add_base(1, 0, 0, HALF_N)
+        store_result(1, 0)
+        add_base(1, 1, 0, mid)
         interleave(scopy, res[1], 0, mid)
-        weigh(1, mid, HALF_N)
-        quantize(res[0], mid, HALF_N, res_scales, mid)
+        quantize(res[0], 0, HALF_N, res_scales, 0)
         store_words(nc.sync, 0, 0, HALF_N)
-        add_base(1, mid, HALF_N)
-        store_result(1, mid, HALF_N)
-        quantize(res[1], 0, mid, res_scales, HALF_N)
-        interleave(vcopy, res[1], mid, mid + OUT_ON_VECTOR)
-        interleave(scopy, res[1], mid + OUT_ON_VECTOR, HALF_N)
-        store_words(nc.scalar, 1, 0, mid)
-        quantize(res[1], mid, HALF_N, res_scales, HALF_N + mid)
-        store_words(nc.scalar, 1, mid, HALF_N)
+        add_base(1, 1, mid, HALF_N)
+        store_result(1, 1)
+        interleave(vcopy, res[1], mid, HALF_N)
+        quantize(res[1], 0, HALF_N, res_scales, HALF_N)
+        store_words(nc.scalar, 1, 0, HALF_N)
         store_scales((nc.sync, nc.scalar))

@@ -4,6 +4,7 @@ import concourse.mybir as mybir
 
 G, D, M, N = 2, 256, 256, 512
 FLOPS = 4 * 2 * G * D * M * N
+OUT_SCALE = 512.0
 
 F32 = mybir.dt.float32
 BF16 = mybir.dt.bfloat16
@@ -19,10 +20,14 @@ PACK = 4
 ROWS = D // PACK
 HALVES = M // P
 QUAD = 32
-HALF_N = N // 2
-X_ON_VECTOR = 344
-DX_ON_GPSIMD = 240
-OUT_ON_VECTOR = 88
+SCALE_ROWS = 4
+COL_HALVES = 2
+HALF_N = N // COL_HALVES
+QUARTER_N = HALF_N // 2
+PAIRS = PACK // 2
+
+WIDE_ON_VECTOR = 288
+W1_ON_VECTOR = 64
 
 
 def tile_rows_pl_tnrowsoft_kernel(tc, x, w1, w2, tp, dx, og, base, out_0, out_1, out_2):
@@ -37,45 +42,47 @@ def tile_rows_pl_tnrowsoft_kernel(tc, x, w1, w2, tp, dx, og, base, out_0, out_1,
 
         def operand(name, width):
             return {
-                "raw": sbuf(name + "_raw", [P, PACK, width], F32),
-                "packed": sbuf(name + "_packed", [P, width, PACK], BF16),
+                "values": sbuf(name + "_values", [P, PACK, width], F32),
+                "rounded": sbuf(name + "_rounded", [P, width, PACK], BF16),
                 "codes": sbuf(name + "_codes", [P, width], U32),
                 "scales": sbuf(name + "_scales", [P, width], U8),
             }
 
         def load(op, src):
-            nc.sync.dma_start(out=op["raw"][:], in_=src.rearrange("g (q j) c -> (g q) j c", j=PACK))
+            nc.sync.dma_start(out=op["values"][:], in_=src.rearrange("g (q t) c -> (g q) t c", t=PACK))
 
         def interleave(copy, op, lo, hi):
             copy(
-                out=op["packed"][:, lo:hi, :].rearrange("p (c i) j -> p c j i", i=2),
-                in_=op["raw"][:, :, lo:hi].rearrange("p j (c i) -> p c j i", i=2),
+                out=op["rounded"][:, lo:hi, :].rearrange("p (c i) t -> p c t i", i=2),
+                in_=op["values"][:, :, lo:hi].rearrange("p t (c i) -> p c t i", i=2),
             )
 
-        def quantize(op, lo, hi, scales, at):
+        def quantize(op, lo, hi):
             nc.vector.quantize_mx(
                 out=op["codes"][:, lo:hi].bitcast(FP8X4),
-                scales=scales[:, at : at + hi - lo],
-                in_=op["packed"][:, lo:hi, :].rearrange("p c j -> p (c j)"),
+                scales=op["scales"][:, lo:hi],
+                in_=op["rounded"][:, lo:hi, :].rearrange("p c t -> p (c t)"),
             )
 
-        def product(bank, w, a, g, h):
+        def product(bank, weights, moving, g, h):
             rows = slice(ROWS * g, ROWS * (g + 1))
-            cols = slice(P * h, P * (h + 1))
+            features = slice(P * h, P * (h + 1))
             nc.tensor.matmul_mx(
                 out=bank[:],
-                lhsT=w["codes"][rows, cols].bitcast(FP8X4),
-                lhsT_scale=w["scales"][rows, cols],
-                rhs=a["codes"][rows, :].bitcast(FP8X4),
-                rhs_scale=a["scales"][rows, :],
+                lhsT=weights["codes"][rows, features].bitcast(FP8X4),
+                lhsT_scale=weights["scales"][rows, features],
+                rhs=moving["codes"][rows, :].bitcast(FP8X4),
+                rhs_scale=moving["scales"][rows, :],
                 start=True,
                 stop=True,
             )
 
-        xo, dxo = operand("x", N), operand("dx", N)
-        w1o, w2o = operand("w1", M), operand("w2", M)
-        banks = [[ps.tile([P, N], F32, name="bank_%d_%d" % (g, b)) for b in range(4)] for g in range(G)]
-        tiles = [(g, h) for h in range(HALVES) for g in range(G)]
+        x_op, dx_op = operand("x", N), operand("dx", N)
+        w1_op, w2_op = operand("w1", M), operand("w2", M)
+        banks = [[ps.tile([P, N], F32, name="bank_%d_%d" % (g, b)) for b in range(2 * HALVES)] for g in range(G)]
+        w1_bank = {(g, h): banks[g][h] for g in range(G) for h in range(HALVES)}
+        w2_bank = {(g, h): banks[g][HALVES + h] for g in range(G) for h in range(HALVES)}
+        feature_tiles = [(g, h) for h in range(HALVES) for g in range(G)]
 
         vec_rows = sbuf("vec_rows", [P, P], F32)
         vec_cols = sbuf("vec_cols", [P, G, HALVES, QUAD], F32)
@@ -85,65 +92,59 @@ def tile_rows_pl_tnrowsoft_kernel(tc, x, w1, w2, tp, dx, og, base, out_0, out_1,
         neg_max = sbuf("neg_max", [P, HALVES, G], F32)
         zs = [sbuf("zs%d" % h, [P, G], F32) for h in range(HALVES)]
         inv_zs = [sbuf("inv_zs%d" % h, [P, G], F32) for h in range(HALVES)]
-        mean_tz = sbuf("mean_tz", [P, HALVES, G], F32)
-        base_sb = sbuf("base_sb", [P, PACK, N], F32)
-        p_rows = sbuf("p_rows", [P, PACK, N], F32)
+        mean = sbuf("mean", [P, HALVES, G], F32)
+        base_packed = sbuf("base_packed", [P, PACK, N], F32)
+        p_packed = sbuf("p_packed", [P, PACK, N], F32)
         work = {}
-        for g, h in tiles:
-            for name in ("s", "p", "u", "z2", "t2"):
+        for g, h in feature_tiles:
+            for name in ("neg_score", "p", "mean_terms", "z2_scaled", "centred"):
                 work[name, g, h] = sbuf("%s_%d_%d" % (name, g, h), [P, N], F32)
-            for c in range(2):
-                work["t3", g, h, c] = sbuf("t3_%d_%d_%d" % (g, h, c), [P, HALF_N], F32)
-        res = []
-        for h in range(2):
-            res.append({
-                "t3": sbuf("res_t3%d" % h, [P, PACK, HALF_N], F32),
-                "t4": sbuf("res_t4%d" % h, [P, PACK, HALF_N], F32),
-                "raw": sbuf("res_raw%d" % h, [P, PACK, HALF_N], F32),
-                "packed": sbuf("res_packed%d" % h, [P, HALF_N, PACK], BF16),
-                "codes": sbuf("res_codes%d" % h, [P, HALF_N], U32),
+            for c in range(COL_HALVES):
+                work["slope", g, h, c] = sbuf("slope_%d_%d_%d" % (g, h, c), [P, HALF_N], F32)
+        result = []
+        for c in range(COL_HALVES):
+            result.append({
+                "slope": sbuf("result_slope%d" % c, [P, PACK, HALF_N], F32),
+                "change": sbuf("result_change%d" % c, [P, PACK, HALF_N], F32),
+                "values": sbuf("result_values%d" % c, [P, PACK, HALF_N], F32),
+                "rounded": sbuf("result_rounded%d" % c, [P, HALF_N, PACK], BF16),
+                "codes": sbuf("result_codes%d" % c, [P, HALF_N], U32),
             })
-        res_scales = sbuf("res_scales", [P, HALVES * HALF_N], U8)
+        result_scales = sbuf("result_scales", [P, N], U8)
 
         nc.gpsimd.memset(vec_rows[:], 0.0)
-        load(xo, x)
-        load(w1o, w1)
+        load(x_op, x)
+        load(w1_op, w1)
         for k, vec in enumerate((tp, og)):
             nc.sync.dma_start(
                 out=vec_rows[k:P:QUAD, :].rearrange("q (t i) -> q t i", i=QUAD),
                 in_=vec.rearrange("g (h q i) o -> q (g h) (i o)", h=HALVES, i=QUAD),
             )
-        load(w2o, w2)
-        load(dxo, dx)
-        nc.sync.dma_start(out=base_sb[:], in_=base.rearrange("g (q t) n -> (g q) t n", t=PACK))
+        load(w2_op, w2)
+        load(dx_op, dx)
+        nc.sync.dma_start(out=base_packed[:], in_=base.rearrange("g (q t) n -> (g q) t n", t=PACK))
 
-        vcopy, scopy = nc.vector.tensor_copy, nc.scalar.copy
+        vector_copy, scalar_copy = nc.vector.tensor_copy, nc.scalar.copy
 
-        def gcopy(out, in_):
-            nc.gpsimd.tensor_scalar(out=out, in0=in_, scalar1=1.0, scalar2=0.0, op0=ALU.mult, op1=ALU.add)
-
-        def interleave_gpsimd(op, lo, hi):
-            gcopy(op["packed"][:, lo:hi, :], op["raw"][:, :, lo:hi].rearrange("p j c -> p c j"))
-
-        def row_constants():
+        def feature_constants():
             nc.vector.transpose(out=vec_cols[:].rearrange("p g h i -> p (g h i)"), in_=vec_rows[:])
             tp_cols = vec_cols[:, :, :, 0].rearrange("p g h -> p h g")
             og_cols = vec_cols[:, :, :, 1].rearrange("p g h -> p h g")
             nc.vector.tensor_scalar(out=neg_tp[:], in0=tp_cols, scalar1=-1.0, scalar2=None, op0=ALU.mult)
-            nc.vector.tensor_scalar(out=gains[:, :, 0, :], in0=og_cols, scalar1=float(N), scalar2=None, op0=ALU.mult)
+            nc.vector.tensor_scalar(out=gains[:, :, 0, :], in0=og_cols, scalar1=OUT_SCALE, scalar2=None, op0=ALU.mult)
             nc.vector.scalar_tensor_tensor(
-                out=gains[:, :, 1, :], in0=og_cols, scalar=float(N), in1=tp_cols, op0=ALU.mult, op1=ALU.mult
+                out=gains[:, :, 1, :], in0=og_cols, scalar=OUT_SCALE, in1=tp_cols, op0=ALU.mult, op1=ALU.mult
             )
 
         def row_max(g, h):
             nc.vector.tensor_scalar(
-                out=work["s", g, h][:], in0=banks[g][h][:], scalar1=neg_tp[:, h, g : g + 1], scalar2=None,
+                out=work["neg_score", g, h][:], in0=w1_bank[g, h][:], scalar1=neg_tp[:, h, g : g + 1], scalar2=None,
                 op0=ALU.mult, op1=ALU.min, accum_out=neg_max[:, h, g : g + 1],
             )
 
         def exponential(g, h):
             nc.scalar.activation(
-                out=work["p", g, h][:], in_=work["s", g, h][:], func=ACT.Exp, scale=-1.0,
+                out=work["p", g, h][:], in_=work["neg_score", g, h][:], func=ACT.Exp, scale=-1.0,
                 bias=neg_max[:, h, g : g + 1], accum_out=zs[h][:, g : g + 1],
             )
 
@@ -156,146 +157,156 @@ def tile_rows_pl_tnrowsoft_kernel(tc, x, w1, w2, tp, dx, og, base, out_0, out_1,
                 op=ALU.mult,
             )
 
-        def mean(g, h, b=0):
+        def row_mean(g, h):
             nc.vector.scalar_tensor_tensor(
-                out=work["u", g, h][:], in0=banks[g][b + h][:], scalar=inv_zs[h][:, g : g + 1],
-                in1=work["p", g, h][:], op0=ALU.mult, op1=ALU.mult, accum_out=mean_tz[:, h, g : g + 1],
+                out=work["mean_terms", g, h][:], in0=w1_bank[g, h][:], scalar=inv_zs[h][:, g : g + 1],
+                in1=work["p", g, h][:], op0=ALU.mult, op1=ALU.mult, accum_out=mean[:, h, g : g + 1],
             )
 
         def scale_z2(g, h):
             nc.scalar.activation(
-                out=work["z2", g, h][:], in_=banks[g][2 + h][:], func=ACT.Copy, scale=coef[h][:, 1, g : g + 1]
+                out=work["z2_scaled", g, h][:], in_=w2_bank[g, h][:], func=ACT.Copy, scale=coef[h][:, 1, g : g + 1]
             )
 
-        def step2(g, h, lo, hi):
-            cols = slice(lo, hi)
-            nc.vector.scalar_tensor_tensor(
-                out=work["t2", g, h][:, cols], in0=banks[g][h][:, cols], scalar=mean_tz[:, h, g : g + 1],
-                in1=work["z2", g, h][:, cols], op0=ALU.subtract, op1=ALU.mult,
-            )
-
-        def step3(g, h, c):
+        def centre(g, h, c):
             cols = slice(HALF_N * c, HALF_N * (c + 1))
             nc.vector.scalar_tensor_tensor(
-                out=work["t3", g, h, c][:], in0=banks[g][2 + h][:, cols], scalar=coef[h][:, 0, g : g + 1],
-                in1=work["t2", g, h][:, cols], op0=ALU.mult, op1=ALU.add,
+                out=work["centred", g, h][:, cols], in0=w1_bank[g, h][:, cols], scalar=mean[:, h, g : g + 1],
+                in1=work["z2_scaled", g, h][:, cols], op0=ALU.subtract, op1=ALU.mult,
             )
 
-        def regroup(queue, dst, src, g, h):
+        def add_tz2(g, h, c):
+            cols = slice(HALF_N * c, HALF_N * (c + 1))
+            nc.vector.scalar_tensor_tensor(
+                out=work["slope", g, h, c][:], in0=w2_bank[g, h][:, cols], scalar=coef[h][:, 0, g : g + 1],
+                in1=work["centred", g, h][:, cols], op0=ALU.mult, op1=ALU.add,
+            )
+
+        queues = (nc.sync, nc.scalar)
+
+        def regroup(dst, src, g, h):
             at = ROWS * g + QUAD * h
-            queue.dma_start(out=dst[at : at + QUAD, :, :], in_=src[:])
+            queues[g].dma_start(out=dst[at : at + QUAD, :, :], in_=src[:])
+
+        def regroup_p(g, h):
+            regroup(p_packed, work["p", g, h], g, h)
 
         def weigh(c, pair):
             places = slice(2 * pair, 2 * pair + 2)
             nc.vector.tensor_tensor(
-                out=res[c]["t4"][:, places, :], in0=res[c]["t3"][:, places, :],
-                in1=p_rows[:, places, HALF_N * c : HALF_N * (c + 1)], op=ALU.mult,
+                out=result[c]["change"][:, places, :], in0=result[c]["slope"][:, places, :],
+                in1=p_packed[:, places, HALF_N * c : HALF_N * (c + 1)], op=ALU.mult,
             )
 
         def add_base(c, pair, lo, hi):
             places = slice(2 * pair, 2 * pair + 2)
             nc.vector.tensor_tensor(
-                out=res[c]["raw"][:, places, lo:hi], in0=res[c]["t4"][:, places, lo:hi],
-                in1=base_sb[:, places, HALF_N * c + lo : HALF_N * c + hi], op=ALU.add,
+                out=result[c]["values"][:, places, lo:hi], in0=result[c]["change"][:, places, lo:hi],
+                in1=base_packed[:, places, HALF_N * c + lo : HALF_N * c + hi], op=ALU.add,
             )
 
-        def store_result(c, pair):
+        def store_values(c, pair):
             cols = slice(HALF_N * c, HALF_N * (c + 1))
             places = slice(2 * pair, 2 * pair + 2)
             nc.sync.dma_start(
-                out=out_0.rearrange("(p t) n -> p t n", t=PACK)[:, places, cols], in_=res[c]["raw"][:, places, :]
+                out=out_0.rearrange("(p t) n -> p t n", t=PACK)[:, places, cols], in_=result[c]["values"][:, places, :]
             )
+
+        def quantize_result(c):
+            quantize(dict(result[c], scales=result_scales[:, HALF_N * c : HALF_N * (c + 1)]), 0, HALF_N)
 
         words_out = out_1.rearrange("v p n u -> (v p) (n u)").bitcast(I32)
         scales_out = out_2.rearrange("v f n -> (v f) n").bitcast(I32)
 
-        def store_words(queue, c, lo, hi):
-            queue.dma_start(
-                out=words_out[:, HALF_N * c + lo : HALF_N * c + hi], in_=res[c]["codes"][:, lo:hi].bitcast(I32)
+        def store_words(c):
+            queues[c].dma_start(
+                out=words_out[:, HALF_N * c : HALF_N * (c + 1)], in_=result[c]["codes"][:, 0:HALF_N].bitcast(I32)
             )
 
-        def store_scales(queues):
+        def store_scales():
             for q in range(P // QUAD):
                 queues[q % 2].dma_start(
-                    out=scales_out[4 * q : 4 * q + 4, :], in_=res_scales[QUAD * q : QUAD * q + 4, :].bitcast(I32)
+                    out=scales_out[SCALE_ROWS * q : SCALE_ROWS * (q + 1), :],
+                    in_=result_scales[QUAD * q : QUAD * q + SCALE_ROWS, :].bitcast(I32),
                 )
 
-        interleave(vcopy, xo, 0, 288)
-        interleave(scopy, xo, 288, N)
-        quantize(xo, 0, HALF_N, xo["scales"], 0)
-        interleave(vcopy, w1o, 0, 64)
-        interleave(scopy, w1o, 64, P)
-        interleave(scopy, w1o, P, M)
-        quantize(xo, HALF_N, N, xo["scales"], HALF_N)
-        quantize(w1o, 0, P, w1o["scales"], 0)
+        interleave(vector_copy, x_op, 0, WIDE_ON_VECTOR)
+        interleave(scalar_copy, x_op, WIDE_ON_VECTOR, N)
+        quantize(x_op, 0, HALF_N)
+        interleave(vector_copy, w1_op, 0, W1_ON_VECTOR)
+        interleave(scalar_copy, w1_op, W1_ON_VECTOR, P)
+        interleave(scalar_copy, w1_op, P, M)
+        quantize(x_op, HALF_N, N)
+        quantize(w1_op, 0, P)
         for g in range(G):
-            product(banks[g][0], w1o, xo, g, 0)
-        row_constants()
-        quantize(w1o, P, M, w1o["scales"], P)
+            product(w1_bank[g, 0], w1_op, x_op, g, 0)
+        feature_constants()
+        quantize(w1_op, P, M)
         for g in range(G):
-            product(banks[g][1], w1o, xo, g, 1)
+            product(w1_bank[g, 1], w1_op, x_op, g, 1)
 
-        interleave(scopy, w2o, 0, M)
+        interleave(scalar_copy, w2_op, 0, M)
         row_max(0, 0)
         row_max(1, 0)
-        quantize(w2o, 0, M, w2o["scales"], 0)
-        for g, h in tiles:
-            product(banks[g][2 + h], w2o, xo, g, h)
+        quantize(w2_op, 0, M)
+        for g, h in feature_tiles:
+            product(w2_bank[g, h], w2_op, x_op, g, h)
         exponential(0, 0)
-        regroup(nc.sync, p_rows, work["p", 0, 0], 0, 0)
+        regroup_p(0, 0)
         row_max(0, 1)
-        interleave(vcopy, dxo, 0, 288)
-        interleave(scopy, dxo, 288, N)
+        interleave(vector_copy, dx_op, 0, WIDE_ON_VECTOR)
+        interleave(scalar_copy, dx_op, WIDE_ON_VECTOR, N)
         exponential(1, 0)
-        quantize(dxo, 0, N, dxo["scales"], 0)
+        quantize(dx_op, 0, N)
         row_max(1, 1)
-        for g, h in tiles:
-            product(banks[g][h], w1o, dxo, g, h)
+        for g, h in feature_tiles:
+            product(w1_bank[g, h], w1_op, dx_op, g, h)
         reciprocal(0)
         exponential(0, 1)
-        regroup(nc.scalar, p_rows, work["p", 1, 0], 1, 0)
-        regroup(nc.sync, p_rows, work["p", 0, 1], 0, 1)
+        regroup_p(1, 0)
+        regroup_p(0, 1)
         exponential(1, 1)
+
         coefficients(0)
-        mean(0, 0)
+        row_mean(0, 0)
         reciprocal(1)
-        mean(1, 0)
+        row_mean(1, 0)
         coefficients(1)
         for g in range(G):
             scale_z2(g, 0)
-        regroup(nc.scalar, p_rows, work["p", 1, 1], 1, 1)
+        regroup_p(1, 1)
         for g in range(G):
-            mean(g, 1)
+            row_mean(g, 1)
             scale_z2(g, 1)
-        for g, h in tiles:
-            product(banks[g][2 + h], w2o, dxo, g, h)
+        for g, h in feature_tiles:
+            product(w2_bank[g, h], w2_op, dx_op, g, h)
 
-        queues = (nc.sync, nc.scalar)
-        for c in range(2):
-            for g, h in tiles:
-                step2(g, h, HALF_N * c, HALF_N * (c + 1))
-            for g, h in tiles:
-                step3(g, h, c)
-                regroup(queues[g], res[c]["t3"], work["t3", g, h, c], g, h)
+        for c in range(COL_HALVES):
+            for h in range(HALVES):
+                for g in range(G):
+                    centre(g, h, c)
+                for g in range(G):
+                    add_tz2(g, h, c)
+                    regroup(result[c]["slope"], work["slope", g, h, c], g, h)
 
-        mid = HALF_N // 2
-        for pair in range(2):
+        for pair in range(PAIRS):
             weigh(0, pair)
-        for pair in range(2):
+        for pair in range(PAIRS):
             add_base(0, pair, 0, HALF_N)
-            store_result(0, pair)
-        interleave(scopy, res[0], 0, HALF_N)
-        for pair in range(2):
+            store_values(0, pair)
+        interleave(scalar_copy, result[0], 0, HALF_N)
+
+        for pair in range(PAIRS):
             weigh(1, pair)
         add_base(1, 0, 0, HALF_N)
-        store_result(1, 0)
-        add_base(1, 1, 0, mid)
-        interleave(scopy, res[1], 0, mid)
-        quantize(res[0], 0, HALF_N, res_scales, 0)
-        store_words(nc.sync, 0, 0, HALF_N)
-        add_base(1, 1, mid, HALF_N)
-        store_result(1, 1)
-        interleave(vcopy, res[1], mid, HALF_N)
-        quantize(res[1], 0, HALF_N, res_scales, HALF_N)
-        store_words(nc.scalar, 1, 0, HALF_N)
-        store_scales((nc.sync, nc.scalar))
+        store_values(1, 0)
+        add_base(1, 1, 0, QUARTER_N)
+        interleave(scalar_copy, result[1], 0, QUARTER_N)
+        quantize_result(0)
+        store_words(0)
+        add_base(1, 1, QUARTER_N, HALF_N)
+        store_values(1, 1)
+        interleave(vector_copy, result[1], QUARTER_N, HALF_N)
+        quantize_result(1)
+        store_words(1)
+        store_scales()

from contextlib import ExitStack

import concourse.mybir as mybir

G, D, M, N = 2, 256, 256, 512
FLOPS = 4 * 2 * G * D * M * N
OUT_SCALE = 512.0

F32 = mybir.dt.float32
BF16 = mybir.dt.bfloat16
U32 = mybir.dt.uint32
I32 = mybir.dt.int32
U8 = mybir.dt.uint8
FP8X4 = mybir.dt.float8_e4m3fn_x4
ALU = mybir.AluOpType
ACT = mybir.ActivationFunctionType

P = 128
PACK = 4
ROWS = D // PACK
HALVES = M // P
QUAD = 32
SCALE_ROWS = 4
COL_HALVES = 2
HALF_N = N // COL_HALVES
QUARTER_N = HALF_N // 2
PAIRS = PACK // 2

WIDE_ON_VECTOR = 288
W1_ON_VECTOR = 64


def tile_rows_pl_tnrowsoft_kernel(tc, x, w1, w2, tp, dx, og, base, out_0, out_1, out_2):
    nc = tc.nc
    with ExitStack() as ctx:
        sb = ctx.enter_context(tc.tile_pool(name="sb", bufs=1))
        ps = ctx.enter_context(tc.psum_pool(name="ps", bufs=1))
        ctx.enter_context(tc.manual_schedule())

        def sbuf(name, shape, dtype):
            return sb.tile(shape, dtype, name=name, align_bytes=64)

        def operand(name, width):
            return {
                "values": sbuf(name + "_values", [P, PACK, width], F32),
                "rounded": sbuf(name + "_rounded", [P, width, PACK], BF16),
                "codes": sbuf(name + "_codes", [P, width], U32),
                "scales": sbuf(name + "_scales", [P, width], U8),
            }

        def load(op, src):
            nc.sync.dma_start(out=op["values"][:], in_=src.rearrange("g (q t) c -> (g q) t c", t=PACK))

        def interleave(copy, op, lo, hi):
            copy(
                out=op["rounded"][:, lo:hi, :].rearrange("p (c i) t -> p c t i", i=2),
                in_=op["values"][:, :, lo:hi].rearrange("p t (c i) -> p c t i", i=2),
            )

        def quantize(op, lo, hi):
            nc.vector.quantize_mx(
                out=op["codes"][:, lo:hi].bitcast(FP8X4),
                scales=op["scales"][:, lo:hi],
                in_=op["rounded"][:, lo:hi, :].rearrange("p c t -> p (c t)"),
            )

        def product(bank, weights, moving, g, h):
            rows = slice(ROWS * g, ROWS * (g + 1))
            features = slice(P * h, P * (h + 1))
            nc.tensor.matmul_mx(
                out=bank[:],
                lhsT=weights["codes"][rows, features].bitcast(FP8X4),
                lhsT_scale=weights["scales"][rows, features],
                rhs=moving["codes"][rows, :].bitcast(FP8X4),
                rhs_scale=moving["scales"][rows, :],
                start=True,
                stop=True,
            )

        x_op, dx_op = operand("x", N), operand("dx", N)
        w1_op, w2_op = operand("w1", M), operand("w2", M)
        banks = [[ps.tile([P, N], F32, name="bank_%d_%d" % (g, b)) for b in range(2 * HALVES)] for g in range(G)]
        w1_bank = {(g, h): banks[g][h] for g in range(G) for h in range(HALVES)}
        w2_bank = {(g, h): banks[g][HALVES + h] for g in range(G) for h in range(HALVES)}
        feature_tiles = [(g, h) for h in range(HALVES) for g in range(G)]

        vec_rows = sbuf("vec_rows", [P, P], F32)
        vec_cols = sbuf("vec_cols", [P, G, HALVES, QUAD], F32)
        neg_tp = sbuf("neg_tp", [P, HALVES, G], F32)
        gains = sbuf("gains", [P, HALVES, 2, G], F32)
        coef = [sbuf("coef%d" % h, [P, 2, G], F32) for h in range(HALVES)]
        neg_max = sbuf("neg_max", [P, HALVES, G], F32)
        zs = [sbuf("zs%d" % h, [P, G], F32) for h in range(HALVES)]
        inv_zs = [sbuf("inv_zs%d" % h, [P, G], F32) for h in range(HALVES)]
        mean = sbuf("mean", [P, HALVES, G], F32)
        base_packed = sbuf("base_packed", [P, PACK, N], F32)
        p_packed = sbuf("p_packed", [P, PACK, N], F32)
        work = {}
        for g, h in feature_tiles:
            for name in ("neg_score", "p", "mean_terms", "z2_scaled", "centred"):
                work[name, g, h] = sbuf("%s_%d_%d" % (name, g, h), [P, N], F32)
            for c in range(COL_HALVES):
                work["slope", g, h, c] = sbuf("slope_%d_%d_%d" % (g, h, c), [P, HALF_N], F32)
        result = []
        for c in range(COL_HALVES):
            result.append({
                "slope": sbuf("result_slope%d" % c, [P, PACK, HALF_N], F32),
                "change": sbuf("result_change%d" % c, [P, PACK, HALF_N], F32),
                "values": sbuf("result_values%d" % c, [P, PACK, HALF_N], F32),
                "rounded": sbuf("result_rounded%d" % c, [P, HALF_N, PACK], BF16),
                "codes": sbuf("result_codes%d" % c, [P, HALF_N], U32),
            })
        result_scales = sbuf("result_scales", [P, N], U8)

        nc.gpsimd.memset(vec_rows[:], 0.0)
        load(x_op, x)
        load(w1_op, w1)
        for k, vec in enumerate((tp, og)):
            nc.sync.dma_start(
                out=vec_rows[k:P:QUAD, :].rearrange("q (t i) -> q t i", i=QUAD),
                in_=vec.rearrange("g (h q i) o -> q (g h) (i o)", h=HALVES, i=QUAD),
            )
        load(w2_op, w2)
        load(dx_op, dx)
        nc.sync.dma_start(out=base_packed[:], in_=base.rearrange("g (q t) n -> (g q) t n", t=PACK))

        vector_copy, scalar_copy = nc.vector.tensor_copy, nc.scalar.copy

        def feature_constants():
            nc.vector.transpose(out=vec_cols[:].rearrange("p g h i -> p (g h i)"), in_=vec_rows[:])
            tp_cols = vec_cols[:, :, :, 0].rearrange("p g h -> p h g")
            og_cols = vec_cols[:, :, :, 1].rearrange("p g h -> p h g")
            nc.vector.tensor_scalar(out=neg_tp[:], in0=tp_cols, scalar1=-1.0, scalar2=None, op0=ALU.mult)
            nc.vector.tensor_scalar(out=gains[:, :, 0, :], in0=og_cols, scalar1=OUT_SCALE, scalar2=None, op0=ALU.mult)
            nc.vector.scalar_tensor_tensor(
                out=gains[:, :, 1, :], in0=og_cols, scalar=OUT_SCALE, in1=tp_cols, op0=ALU.mult, op1=ALU.mult
            )

        def row_max(g, h):
            nc.vector.tensor_scalar(
                out=work["neg_score", g, h][:], in0=w1_bank[g, h][:], scalar1=neg_tp[:, h, g : g + 1], scalar2=None,
                op0=ALU.mult, op1=ALU.min, accum_out=neg_max[:, h, g : g + 1],
            )

        def exponential(g, h):
            nc.scalar.activation(
                out=work["p", g, h][:], in_=work["neg_score", g, h][:], func=ACT.Exp, scale=-1.0,
                bias=neg_max[:, h, g : g + 1], accum_out=zs[h][:, g : g + 1],
            )

        def reciprocal(h):
            nc.vector.reciprocal(out=inv_zs[h][:], in_=zs[h][:])

        def coefficients(h):
            nc.vector.tensor_tensor(
                out=coef[h][:], in0=gains[:, h, :, :], in1=inv_zs[h][:].unsqueeze(1).to_broadcast([P, 2, G]),
                op=ALU.mult,
            )

        def row_mean(g, h):
            nc.vector.scalar_tensor_tensor(
                out=work["mean_terms", g, h][:], in0=w1_bank[g, h][:], scalar=inv_zs[h][:, g : g + 1],
                in1=work["p", g, h][:], op0=ALU.mult, op1=ALU.mult, accum_out=mean[:, h, g : g + 1],
            )

        def scale_z2(g, h):
            nc.scalar.activation(
                out=work["z2_scaled", g, h][:], in_=w2_bank[g, h][:], func=ACT.Copy, scale=coef[h][:, 1, g : g + 1]
            )

        def centre(g, h, c):
            cols = slice(HALF_N * c, HALF_N * (c + 1))
            nc.vector.scalar_tensor_tensor(
                out=work["centred", g, h][:, cols], in0=w1_bank[g, h][:, cols], scalar=mean[:, h, g : g + 1],
                in1=work["z2_scaled", g, h][:, cols], op0=ALU.subtract, op1=ALU.mult,
            )

        def add_tz2(g, h, c):
            cols = slice(HALF_N * c, HALF_N * (c + 1))
            nc.vector.scalar_tensor_tensor(
                out=work["slope", g, h, c][:], in0=w2_bank[g, h][:, cols], scalar=coef[h][:, 0, g : g + 1],
                in1=work["centred", g, h][:, cols], op0=ALU.mult, op1=ALU.add,
            )

        queues = (nc.sync, nc.scalar)

        def regroup(dst, src, g, h):
            at = ROWS * g + QUAD * h
            queues[g].dma_start(out=dst[at : at + QUAD, :, :], in_=src[:])

        def regroup_p(g, h):
            regroup(p_packed, work["p", g, h], g, h)

        def weigh(c, pair):
            places = slice(2 * pair, 2 * pair + 2)
            nc.vector.tensor_tensor(
                out=result[c]["change"][:, places, :], in0=result[c]["slope"][:, places, :],
                in1=p_packed[:, places, HALF_N * c : HALF_N * (c + 1)], op=ALU.mult,
            )

        def add_base(c, pair, lo, hi):
            places = slice(2 * pair, 2 * pair + 2)
            nc.vector.tensor_tensor(
                out=result[c]["values"][:, places, lo:hi], in0=result[c]["change"][:, places, lo:hi],
                in1=base_packed[:, places, HALF_N * c + lo : HALF_N * c + hi], op=ALU.add,
            )

        def store_values(c, pair):
            cols = slice(HALF_N * c, HALF_N * (c + 1))
            places = slice(2 * pair, 2 * pair + 2)
            nc.sync.dma_start(
                out=out_0.rearrange("(p t) n -> p t n", t=PACK)[:, places, cols], in_=result[c]["values"][:, places, :]
            )

        def quantize_result(c):
            quantize(dict(result[c], scales=result_scales[:, HALF_N * c : HALF_N * (c + 1)]), 0, HALF_N)

        words_out = out_1.rearrange("v p n u -> (v p) (n u)").bitcast(I32)
        scales_out = out_2.rearrange("v f n -> (v f) n").bitcast(I32)

        def store_words(c):
            queues[c].dma_start(
                out=words_out[:, HALF_N * c : HALF_N * (c + 1)], in_=result[c]["codes"][:, 0:HALF_N].bitcast(I32)
            )

        def store_scales():
            for q in range(P // QUAD):
                queues[q % 2].dma_start(
                    out=scales_out[SCALE_ROWS * q : SCALE_ROWS * (q + 1), :],
                    in_=result_scales[QUAD * q : QUAD * q + SCALE_ROWS, :].bitcast(I32),
                )

        interleave(vector_copy, x_op, 0, WIDE_ON_VECTOR)
        interleave(scalar_copy, x_op, WIDE_ON_VECTOR, N)
        quantize(x_op, 0, HALF_N)
        interleave(vector_copy, w1_op, 0, W1_ON_VECTOR)
        interleave(scalar_copy, w1_op, W1_ON_VECTOR, P)
        interleave(scalar_copy, w1_op, P, M)
        quantize(x_op, HALF_N, N)
        quantize(w1_op, 0, P)
        for g in range(G):
            product(w1_bank[g, 0], w1_op, x_op, g, 0)
        feature_constants()
        quantize(w1_op, P, M)
        for g in range(G):
            product(w1_bank[g, 1], w1_op, x_op, g, 1)

        interleave(scalar_copy, w2_op, 0, M)
        row_max(0, 0)
        row_max(1, 0)
        quantize(w2_op, 0, M)
        for g, h in feature_tiles:
            product(w2_bank[g, h], w2_op, x_op, g, h)
        exponential(0, 0)
        regroup_p(0, 0)
        row_max(0, 1)
        interleave(vector_copy, dx_op, 0, WIDE_ON_VECTOR)
        interleave(scalar_copy, dx_op, WIDE_ON_VECTOR, N)
        exponential(1, 0)
        quantize(dx_op, 0, N)
        row_max(1, 1)
        for g, h in feature_tiles:
            product(w1_bank[g, h], w1_op, dx_op, g, h)
        reciprocal(0)
        exponential(0, 1)
        regroup_p(1, 0)
        regroup_p(0, 1)
        exponential(1, 1)

        coefficients(0)
        row_mean(0, 0)
        reciprocal(1)
        row_mean(1, 0)
        coefficients(1)
        for g in range(G):
            scale_z2(g, 0)
        regroup_p(1, 1)
        for g in range(G):
            row_mean(g, 1)
            scale_z2(g, 1)
        for g, h in feature_tiles:
            product(w2_bank[g, h], w2_op, dx_op, g, h)

        for c in range(COL_HALVES):
            for h in range(HALVES):
                for g in range(G):
                    centre(g, h, c)
                for g in range(G):
                    add_tz2(g, h, c)
                    regroup(result[c]["slope"], work["slope", g, h, c], g, h)

        for pair in range(PAIRS):
            weigh(0, pair)
        for pair in range(PAIRS):
            add_base(0, pair, 0, HALF_N)
            store_values(0, pair)
        interleave(scalar_copy, result[0], 0, HALF_N)

        for pair in range(PAIRS):
            weigh(1, pair)
        add_base(1, 0, 0, HALF_N)
        store_values(1, 0)
        add_base(1, 1, 0, QUARTER_N)
        interleave(scalar_copy, result[1], 0, QUARTER_N)
        quantize_result(0)
        store_words(0)
        add_base(1, 1, QUARTER_N, HALF_N)
        store_values(1, 1)
        interleave(vector_copy, result[1], QUARTER_N, HALF_N)
        quantize_result(1)
        store_words(1)
        store_scales()
